import numpy as np
import ml_dtypes


def mxq(x, axis, fmt="e4m3"):
    dtype, down = {"e4m3": (ml_dtypes.float8_e4m3fn, 7), "e5m2": (ml_dtypes.float8_e5m2, 14)}[fmt]
    v = np.moveaxis(np.asarray(x, np.float32).astype(ml_dtypes.bfloat16).astype(np.float64), axis, -1)
    blocks = v.reshape(v.shape[:-1] + (-1, 32))
    amax = np.abs(blocks).max(-1, keepdims=True)
    byte = np.maximum(np.where(amax > 0, np.frexp(amax)[1] - 1 + 127, 0) - down, 1)
    scale = np.exp2(byte - 127.0)
    codes = (blocks / scale).astype(np.float32).astype(dtype).astype(np.float64)
    return np.moveaxis((codes * scale).reshape(v.shape), -1, axis)


WIDE = False


def mx_kscale(k):
    if not WIDE:
        return np.ones(k)
    levels = np.array([10, -10, 5, -5, 0])
    if k % 512:
        return np.exp2(np.random.permutation(np.resize(levels, k // 32))).repeat(32)
    a = np.empty((k // 512, 16))
    for p in range(k // 512):
        a[p, :8] = np.random.permutation(np.resize(levels, 8))
        for g in range(8):
            far = levels[np.abs(levels - a[p, g]) >= 10]
            a[p, g + 8] = far[np.random.randint(len(far))]
    return np.exp2(a.ravel()).repeat(32)


def f64(x):
    return np.asarray(x).astype(np.float64)


def striped(idx):
    return np.tile(np.asarray(idx).reshape(-1, 16).T, (8, 1)).astype(np.uint16)


def unstriped(offs):
    return offs[:16].T.reshape(-1).astype(np.int64)


E2M1 = np.array([0.0, 0.5, 1.0, 1.5, 2.0, 3.0, 4.0, 6.0, -0.0, -0.5, -1.0, -1.5, -2.0, -3.0, -4.0, -6.0])


def pack_weight(w, fmt):
    k, n = w.shape
    w = f64(np.asarray(w, np.float32).astype(ml_dtypes.bfloat16)).reshape(k // 32, 32, n)
    amax = np.abs(w).max(1)
    if fmt == "e4m3":
        byte = np.frexp(amax)[1] - 1 + 127 - 7
    else:
        mant, ex = np.frexp(amax / 6.0)
        byte = np.where(mant > 0.5, ex, ex - 1) + 127
    byte = np.clip(np.where(amax > 0, byte, 1), 1, 254)
    scaled = (w * np.exp2(127.0 - byte)[:, None, :]).reshape(k, n).astype(np.float32)
    by_word = np.ascontiguousarray(scaled.reshape(k // 512, 128, 4, n).transpose(0, 1, 3, 2))
    if fmt == "e4m3":
        words = by_word.astype(ml_dtypes.float8_e4m3fn).view(np.uint8)
    else:
        c = by_word.astype(ml_dtypes.float4_e2m1fn).view(np.uint8) & 0xF
        words = (c[..., 0::2] | (c[..., 1::2] << 4)).reshape(k // 512, 128, 2 * n)
    return np.ascontiguousarray(words), np.ascontiguousarray(byte.astype(np.uint8).reshape(k // 512, 16, n))


def unpack_weight(words, scales, fmt):
    g, _, n = scales.shape
    words = np.ascontiguousarray(words).reshape(g, 128, n, -1)
    if fmt == "e4m3":
        vals = words.view(ml_dtypes.float8_e4m3fn).astype(np.float64)
    else:
        nib = np.empty((g, 128, n, 4), np.uint8)
        nib[..., 0::2] = words & 0xF
        nib[..., 1::2] = words >> 4
        vals = E2M1[nib]
    vals = vals * np.repeat(np.exp2(scales.astype(np.float64) - 127.0), 8, axis=1)[..., None]
    return vals.transpose(0, 1, 3, 2).reshape(g * 512, n)


D, T, I, Q, E, V, K = 512, 2048, 512, 128, 512, 16, 16


def setup_inputs():
    n = np.random.standard_normal
    idx = np.random.permutation(T)[:I]
    fd = mx_kscale(D)
    fi = mx_kscale(I)
    ti = np.ones(T)
    ti[idx] = fi
    keysp = pack_weight(n((D, T)) / fd[:, None], "e2m1")
    return {
        "query": (n((D, Q)) * 1.0 / np.sqrt(D) * fd[:, None]).astype(np.float32),
        "keys_words": keysp[0],
        "keys_scales": keysp[1],
        "lam": (np.random.uniform(0.3, 0.8, (1, Q))).astype(np.float32),
        "os": (np.random.uniform(4.0, 16.0, (1, I)) * fi).astype(np.float32),
        "vals": (n((E, T)) / ti).astype(np.float32),
        "target": (n((Q, E))).astype(np.float32),
        "offs": striped(idx),
    }


def reference(query, keys_words, keys_scales, lam, os, vals, target, offs):
    idx = unstriped(offs)
    keysu = unpack_weight(keys_words, keys_scales, "e2m1")
    keysidxg = keysu[:, idx]
    queryq = mxq(f64(query), 0, "e4m3")
    a0 = keysidxg.T @ queryq
    ag = a0.reshape(I, V, Q // V).max(axis=2)
    ar = np.repeat(ag, Q // V, axis=1)
    s0 = a0 - ar * f64(lam)
    s = s0.T
    p = np.exp(s - np.max(s, axis=1, keepdims=True))
    r = p / np.sum(p, axis=1, keepdims=True)
    rt = r.T
    rg = rt.reshape(I, K, Q // K).sum(axis=2)
    rr = np.repeat(rg, Q // K, axis=1)
    w0 = np.square(rt) / rr
    w = w0.T
    wo1 = w * f64(os)
    wt1 = wo1.T
    vt1 = f64(vals)[:, idx].T
    wt1q = mxq(wt1, 0, "e4m3")
    vt1q = mxq(vt1, 0, "e4m3")
    o = wt1q.T @ vt1q
    rs = f64(target) - o
    k2 = np.sqrt(np.mean(np.square(rs), axis=1, keepdims=True) + 0.5)
    y = rs / k2
    return y

@@ -1,0 +1,243 @@
+from contextlib import ExitStack
+
+import concourse.mybir as mybir
+from concourse.masks import make_identity
+
+D, T, I, Q, E = 512, 2048, 512, 128, 512
+FLOPS = 2 * D * I * Q + 2 * I * Q * E
+
+F32 = mybir.dt.float32
+BF16 = mybir.dt.bfloat16
+I32 = mybir.dt.int32
+U32 = mybir.dt.uint32
+U16 = mybir.dt.uint16
+U8 = mybir.dt.uint8
+FP8X4 = mybir.dt.float8_e4m3fn_x4
+FP4X4 = mybir.dt.float4_e2m1fn_x4
+ALU = mybir.AluOpType
+ACT = mybir.ActivationFunctionType
+AX = mybir.AxisListType
+
+P = 128
+PACK = 4
+GROUP = 8
+GROUPS = Q // GROUP
+PLANES = E // P
+HALF = E // 2
+TINY = 2.0**-100
+
+
+def tile_attend_groupbest_shared_remainder_kernel(tc, query, keys_words, keys_scales, lam, slot_factor, vals, target, offs, out):
+    nc = tc.nc
+    with ExitStack() as ctx:
+        sb = ctx.enter_context(tc.tile_pool(name="sb", bufs=1))
+        ps = ctx.enter_context(tc.psum_pool(name="ps", bufs=1))
+        ps_v = ctx.enter_context(tc.psum_pool(name="ps_v", bufs=2))
+
+        shared = ctx.enter_context(tc.tile_pool(name="shared", bufs=1))
+
+        def tile(shape, dtype, name, tag=None):
+            return sb.tile(shape, dtype, name=name, tag=tag or name, align_bytes=64)
+
+        scale_pool = shared.tile([P, T], U8, offset=0, align_bytes=64)
+        nc.vector.memset(scale_pool[:].bitcast(I32), 0)
+        offsets = tile([P, I // 16], U16, "offsets")
+        nc.sync.dma_start(offsets[:], offs)
+        for quad in range(4):
+            nc.sync.dma_start(
+                scale_pool[32 * quad : 32 * quad + 4, :].bitcast(I32),
+                keys_scales[0, 4 * quad : 4 * quad + 4, :].bitcast(I32),
+            )
+        word_pool = tile([P, T], U16, "word_pool", "pool2")
+        nc.scalar.dma_start(word_pool[:].bitcast(I32), keys_words[0].bitcast(I32))
+        q_raw = tile([P, PACK, Q], F32, "q_raw")
+        nc.scalar.dma_start(q_raw[:], query.rearrange("(p j) q -> p j q", j=PACK))
+        lam_col = tile([P, 1], F32, "lam_col")
+        with nc.allow_non_contiguous_dma(reason="one factor a partition"):
+            nc.gpsimd.dma_start(lam_col[:], lam.rearrange("o q -> q o"))
+        seed = tile([P, 1], F32, "seed", "pool0")
+        nc.vector.memset(seed[:], 0.0)
+        warm = tile([P, 1], F32, "warm")
+        nc.scalar.activation(warm[:], seed[:], ACT.Exp)
+        val_pool = [tile([P, T], F32, "val_pool0", "pool0")]
+        nc.scalar.dma_start(val_pool[0][:], vals[0:P, :])
+
+        ident = tile([P, P], F32, "ident")
+        make_identity(nc, ident[:])
+        half_const = tile([P, 1], F32, "half_const")
+        nc.vector.memset(half_const[:], 0.5)
+        minus_one = tile([P, 1], F32, "minus_one", "picked1")
+        nc.vector.memset(minus_one[:], -1.0)
+        tiny = tile([P, 1], F32, "tiny", "picked2")
+        nc.vector.memset(tiny[:], TINY)
+
+        k_scales = tile([P, I], U8, "k_scales")
+        nc.vector.tensor_copy(k_scales[:], scale_pool[:].indirect(offsets[:]))
+        k_words = [shared.tile([P, I // 2], U16, name="k_words0", offset=0, align_bytes=64), tile([P, I // 2], U16, "k_words1", "pool3")]
+        val_pool.append(shared.tile([P, T], F32, name="val_pool1", offset=1024, align_bytes=64))
+        nc.sync.dma_start(val_pool[1][:], vals[P : 2 * P, :])
+        q_bf = tile([P, Q, PACK], BF16, "q_bf")
+        nc.scalar.copy(q_bf[:], q_raw[:].rearrange("p j q -> p q j"))
+        os_slot = tile([P, PACK], F32, "os_slot", "q_raw")
+        nc.sync.dma_start(os_slot[:], slot_factor.rearrange("o (p t) -> p (o t)", t=PACK))
+        q_codes = tile([P, Q], U32, "q_codes")
+        q_scales = tile([P, Q], U8, "q_scales")
+        nc.vector.tensor_copy(k_words[0][:], word_pool[:].indirect(offsets[:, 0:16]))
+        nc.vector.quantize_mx(out=q_codes[:].bitcast(FP8X4), scales=q_scales[:], in_=q_bf[:].rearrange("p q j -> p (q j)"))
+        nc.vector.tensor_copy(k_words[1][:], word_pool[:].indirect(offsets[:, 16:32]))
+        val_pool.append(tile([P, T], F32, "val_pool2", "pool2"))
+        nc.sync.dma_start(val_pool[2][:], vals[2 * P : 3 * P, :])
+
+        lam_row = ps.tile([P, Q], F32)
+        nc.tensor.transpose(lam_row[:], lam_col[:].to_broadcast([P, P]), ident[:])
+
+        a_ps, a_sb, neg_best, cut = [], [], [], []
+        for h in range(2):
+            a_ps.append(ps.tile([P, 2, Q], F32, name=f"a_ps{h}", tag=f"half{h}"))
+            for r in range(2):
+                nc.tensor.matmul_mx(
+                    out=a_ps[h][:, r, :],
+                    lhsT=k_words[h][:, r * P : (r + 1) * P].bitcast(FP4X4),
+                    lhsT_scale=k_scales[:, (2 * h + r) * P : (2 * h + r + 1) * P],
+                    rhs=q_codes[:].bitcast(FP8X4),
+                    rhs_scale=q_scales[:],
+                    start=True,
+                    stop=True,
+                )
+        val_pool.append(tile([P, T], F32, "val_pool3", "pool3"))
+        nc.sync.dma_start(val_pool[3][:], vals[3 * P : 4 * P, :])
+        for h in range(2):
+            neg_best.append(tile([P, 2, GROUPS], F32, f"neg_best{h}", "picked0" if h == 1 else None))
+            nc.vector.tensor_reduce(
+                neg_best[h][:], a_ps[h][:].rearrange("p r (g j) -> p r g j", j=GROUP), AX.X, ALU.max, negate=True
+            )
+            a_sb.append(tile([P, 2, Q], F32, f"a_sb{h}"))
+            nc.scalar.copy(a_sb[h][:], a_ps[h][:])
+        for h in range(2):
+            cut.append(tile([P, 2, GROUPS, GROUP], F32, f"cut{h}"))
+            nc.vector.tensor_tensor(
+                cut[h][:],
+                neg_best[h][:].unsqueeze(3).to_broadcast([P, 2, GROUPS, GROUP]),
+                lam_row[:].rearrange("p (g j) -> p g j", j=GROUP).unsqueeze(1).to_broadcast([P, 2, GROUPS, GROUP]),
+                ALU.mult,
+            )
+        s_ps = ps.tile([P, I], F32)
+        for h in range(2):
+            for r in range(2):
+                cols = slice((2 * h + r) * P, (2 * h + r + 1) * P)
+                nc.tensor.matmul(s_ps[:, cols], a_sb[h][:, r, :], ident[:], start=(h + r == 0), stop=False, is_transpose=True)
+            for r in range(2):
+                cols = slice((2 * h + r) * P, (2 * h + r + 1) * P)
+                nc.tensor.matmul(
+                    s_ps[:, cols],
+                    cut[h][:, r, :, :].rearrange("p g j -> p (g j)"),
+                    ident[:],
+                    start=False,
+                    stop=(h + r == 2),
+                    is_transpose=True,
+                )
+        tgt = tile([P, E], F32, "tgt", "a_sb0")
+        nc.sync.dma_start(tgt[:], target)
+
+        v_bf = sb.tile([P, E, PACK], BF16, align_bytes=64)
+        v_codes = sb.tile([P, E], U32, align_bytes=64)
+        v_scales = sb.tile([P, E], U8, align_bytes=64)
+
+        def gather_values(c):
+            picked = tile([P, I], BF16, f"picked{c}", "pool2" if c == 3 else None)
+            nc.vector.tensor_copy(picked[:], val_pool[c][:].indirect(offsets[:]))
+            pairs = picked[:].bitcast(F32)
+            turned = ps_v.tile([P, 2, P], F32, name="turned")
+            for u in range(2):
+                nc.tensor.transpose(turned[:, u, :], pairs[:, u : I // 2 : 2], ident[:])
+            nc.scalar.copy(
+                v_bf[:, c * P : (c + 1) * P, :].bitcast(F32),
+                turned[:].rearrange("p u e -> p e u"),
+            )
+
+        def quantise_values(c):
+            cols = slice(c * P, (c + 1) * P)
+            nc.vector.quantize_mx(
+                out=v_codes[:, cols].bitcast(FP8X4),
+                scales=v_scales[:, cols],
+                in_=v_bf[:, cols, :].rearrange("p e t -> p (e t)"),
+            )
+
+        gather_values(0)
+
+        neg_max = tile([P, 1], F32, "neg_max", "pool0")
+        neg_s = tile([P, I], F32, "neg_s")
+        nc.vector.tensor_scalar(neg_s[:], s_ps[:], minus_one[:], None, ALU.mult, ALU.min, accum_out=neg_max[:])
+        prob = sb.tile([P, PACK, P], F32)
+        row_sum = sb.tile([P, 1], F32)
+        nc.scalar.activation(
+            prob[:], s_ps[:].rearrange("q (s t) -> q t s", t=PACK), ACT.Exp, bias=neg_max[:], accum_out=row_sum[:]
+        )
+        gather_values(1)
+        row_inv = shared.tile([P, 1], F32, offset=1024, align_bytes=64)
+        nc.vector.reciprocal(row_inv[:], row_sum[:])
+        quantise_values(0)
+        share = sb.tile([P, PACK, P], F32)
+        nc.vector.tensor_scalar(share[:], prob[:], row_inv[:], tiny[:], ALU.mult, ALU.max)
+        share_sq = sb.tile([P, PACK, P], F32)
+        nc.scalar.activation(share_sq[:], prob[:], ACT.Square, scale=row_inv[:])
+        warm_root = sb.tile([P, 1], F32)
+        nc.scalar.activation(warm_root[:], row_inv[:], ACT.Abs_reciprocal_sqrt)
+        r_ps = ps.tile([P, PACK, Q], F32)
+        for t in range(PACK):
+            nc.tensor.transpose(r_ps[:, t, :], share[:, t, :], ident[:])
+        sq_ps = ps.tile([P, PACK, Q], F32)
+        for t in range(PACK):
+            nc.tensor.transpose(sq_ps[:, t, :], share_sq[:, t, :], ident[:])
+        gather_values(2)
+
+        group_sum = tile([P, GROUPS, PACK], F32, "group_sum", "pool2")
+        nc.vector.tensor_reduce(group_sum[:], r_ps[:].rearrange("p t (g j) -> p g t j", j=GROUP), AX.X, ALU.add)
+        group_inv = tile([P, GROUPS, PACK], F32, "group_inv")
+        quantise_values(1)
+        nc.vector.reciprocal(group_inv[:], group_sum[:])
+        gather_values(3)
+        factor = tile([P, GROUPS, PACK], F32, "factor", "pool3")
+        nc.vector.tensor_tensor(factor[:], group_inv[:], os_slot[:].unsqueeze(1).to_broadcast([P, GROUPS, PACK]), ALU.mult)
+        w_bf = tile([P, GROUPS, GROUP, PACK], BF16, "w_bf")
+        nc.vector.tensor_tensor(
+            w_bf[:],
+            sq_ps[:].rearrange("p t (g j) -> p g j t", j=GROUP),
+            factor[:].unsqueeze(2).to_broadcast([P, GROUPS, GROUP, PACK]),
+            ALU.mult,
+        )
+        quantise_values(2)
+        w_codes = sb.tile([P, Q], U32, align_bytes=64)
+        w_scales = sb.tile([P, Q], U8, align_bytes=64)
+        nc.vector.quantize_mx(
+            out=w_codes[:].bitcast(FP8X4), scales=w_scales[:], in_=w_bf[:].rearrange("p g j t -> p (g j t)")
+        )
+        quantise_values(3)
+
+        rest = sb.tile([P, E], F32)
+        junk = sb.tile([P, E], F32)
+        sums = [sb.tile([P, 1], F32, name=f"sums{h}") for h in range(2)]
+        for h in range(2):
+            cols = slice(h * HALF, (h + 1) * HALF)
+            o_ps = ps.tile([P, HALF], F32, name=f"o_ps{h}", tag=f"half{h}")
+            nc.tensor.matmul_mx(
+                out=o_ps[:],
+                lhsT=w_codes[:].bitcast(FP8X4),
+                lhsT_scale=w_scales[:],
+                rhs=v_codes[:, cols].bitcast(FP8X4),
+                rhs_scale=v_scales[:, cols],
+                start=True,
+                stop=True,
+            )
+            nc.vector.tensor_tensor(rest[:, cols], tgt[:, cols], o_ps[:], ALU.subtract)
+            nc.scalar.activation(junk[:, cols], rest[:, cols], ACT.Square, accum_out=sums[h][:])
+            if h == 0:
+                first = sb.tile([P, 1], F32)
+                nc.scalar.activation(first[:], sums[0][:], ACT.Identity, scale=1.0 / E, bias=half_const[:])
+        inv_root = sb.tile([P, 1], F32)
+        nc.scalar.activation(inv_root[:], sums[1][:], ACT.Abs_reciprocal_sqrt, scale=1.0 / E, bias=first[:])
+        res = [sb.tile([P, HALF], F32, name=f"res{h}") for h in range(2)]
+        nc.vector.tensor_scalar(res[0][:], rest[:, :HALF], inv_root[:], None, ALU.mult)
+        nc.sync.dma_start(out[:, :HALF], res[0][:])
+        nc.scalar.activation(res[1][:], rest[:, HALF:], ACT.Copy, scale=inv_root[:])
+        nc.scalar.dma_start(out[:, HALF:], res[1][:])

@@ -34,57 +34,52 @@ def tile_attend_groupbest_shared_remainder_kernel(tc, query, keys_words, keys_sc
         ps = ctx.enter_context(tc.psum_pool(name="ps", bufs=1))
         ps_v = ctx.enter_context(tc.psum_pool(name="ps_v", bufs=2))
 
-        shared = ctx.enter_context(tc.tile_pool(name="shared", bufs=1))
 
         def tile(shape, dtype, name, tag=None):
             return sb.tile(shape, dtype, name=name, tag=tag or name, align_bytes=64)
 
-        scale_pool = shared.tile([P, T], U8, offset=0, align_bytes=64)
-        nc.vector.memset(scale_pool[:].bitcast(I32), 0)
+        scale_pool = tile([P, T], U8, "scale_pool", "pool2")
+        nc.gpsimd.memset(scale_pool[:].bitcast(I32), 0)
         offsets = tile([P, I // 16], U16, "offsets")
         nc.sync.dma_start(offsets[:], offs)
+        lam_col = tile([P, 1], F32, "lam_col")
+        with nc.allow_non_contiguous_dma(reason="one factor a partition"):
+            nc.scalar.dma_start(lam_col[:], lam.rearrange("o q -> q o"))
         for quad in range(4):
             nc.sync.dma_start(
                 scale_pool[32 * quad : 32 * quad + 4, :].bitcast(I32),
                 keys_scales[0, 4 * quad : 4 * quad + 4, :].bitcast(I32),
             )
-        word_pool = tile([P, T], U16, "word_pool", "pool2")
+        word_pool = tile([P, T], U16, "word_pool")
         nc.scalar.dma_start(word_pool[:].bitcast(I32), keys_words[0].bitcast(I32))
         q_raw = tile([P, PACK, Q], F32, "q_raw")
         nc.scalar.dma_start(q_raw[:], query.rearrange("(p j) q -> p j q", j=PACK))
-        lam_col = tile([P, 1], F32, "lam_col")
-        with nc.allow_non_contiguous_dma(reason="one factor a partition"):
-            nc.gpsimd.dma_start(lam_col[:], lam.rearrange("o q -> q o"))
         seed = tile([P, 1], F32, "seed", "pool0")
         nc.vector.memset(seed[:], 0.0)
+        seed_bias = tile([P, 1], F32, "seed_bias", "pool1")
+        nc.vector.memset(seed_bias[:], 0.0)
         warm = tile([P, 1], F32, "warm")
-        nc.scalar.activation(warm[:], seed[:], ACT.Exp)
+        nc.scalar.activation(warm[:], seed[:], ACT.Exp, bias=seed_bias[:])
         val_pool = [tile([P, T], F32, "val_pool0", "pool0")]
-        nc.scalar.dma_start(val_pool[0][:], vals[0:P, :])
+        nc.sync.dma_start(val_pool[0][:], vals[0:P, :])
+        val_pool.append(tile([P, T], F32, "val_pool1", "pool1"))
+        nc.sync.dma_start(val_pool[1][:], vals[P : 2 * P, :])
 
         ident = tile([P, P], F32, "ident")
         make_identity(nc, ident[:])
         half_const = tile([P, 1], F32, "half_const")
         nc.vector.memset(half_const[:], 0.5)
-        minus_one = tile([P, 1], F32, "minus_one", "picked1")
-        nc.vector.memset(minus_one[:], -1.0)
-        tiny = tile([P, 1], F32, "tiny", "picked2")
-        nc.vector.memset(tiny[:], TINY)
 
-        k_scales = tile([P, I], U8, "k_scales")
-        nc.vector.tensor_copy(k_scales[:], scale_pool[:].indirect(offsets[:]))
-        k_words = [shared.tile([P, I // 2], U16, name="k_words0", offset=0, align_bytes=64), tile([P, I // 2], U16, "k_words1", "pool3")]
-        val_pool.append(shared.tile([P, T], F32, name="val_pool1", offset=1024, align_bytes=64))
-        nc.sync.dma_start(val_pool[1][:], vals[P : 2 * P, :])
+        k_words = tile([P, I], U16, "k_words", "pool3")
+        nc.vector.tensor_copy(k_words[:], word_pool[:].indirect(offsets[:]))
         q_bf = tile([P, Q, PACK], BF16, "q_bf")
         nc.scalar.copy(q_bf[:], q_raw[:].rearrange("p j q -> p q j"))
-        os_slot = tile([P, PACK], F32, "os_slot", "q_raw")
-        nc.sync.dma_start(os_slot[:], slot_factor.rearrange("o (p t) -> p (o t)", t=PACK))
         q_codes = tile([P, Q], U32, "q_codes")
         q_scales = tile([P, Q], U8, "q_scales")
-        nc.vector.tensor_copy(k_words[0][:], word_pool[:].indirect(offsets[:, 0:16]))
+        k_scales = [tile([P, I // 2], U8, f"k_scales{h}") for h in range(2)]
+        nc.vector.tensor_copy(k_scales[0][:], scale_pool[:].indirect(offsets[:, 0:16]))
         nc.vector.quantize_mx(out=q_codes[:].bitcast(FP8X4), scales=q_scales[:], in_=q_bf[:].rearrange("p q j -> p (q j)"))
-        nc.vector.tensor_copy(k_words[1][:], word_pool[:].indirect(offsets[:, 16:32]))
+        nc.vector.tensor_copy(k_scales[1][:], scale_pool[:].indirect(offsets[:, 16:32]))
         val_pool.append(tile([P, T], F32, "val_pool2", "pool2"))
         nc.sync.dma_start(val_pool[2][:], vals[2 * P : 3 * P, :])
 
@@ -97,8 +92,8 @@ def tile_attend_groupbest_shared_remainder_kernel(tc, query, keys_words, keys_sc
             for r in range(2):
                 nc.tensor.matmul_mx(
                     out=a_ps[h][:, r, :],
-                    lhsT=k_words[h][:, r * P : (r + 1) * P].bitcast(FP4X4),
-                    lhsT_scale=k_scales[:, (2 * h + r) * P : (2 * h + r + 1) * P],
+                    lhsT=k_words[:, (2 * h + r) * P : (2 * h + r + 1) * P].bitcast(FP4X4),
+                    lhsT_scale=k_scales[h][:, r * P : (r + 1) * P],
                     rhs=q_codes[:].bitcast(FP8X4),
                     rhs_scale=q_scales[:],
                     start=True,
@@ -107,14 +102,14 @@ def tile_attend_groupbest_shared_remainder_kernel(tc, query, keys_words, keys_sc
         val_pool.append(tile([P, T], F32, "val_pool3", "pool3"))
         nc.sync.dma_start(val_pool[3][:], vals[3 * P : 4 * P, :])
         for h in range(2):
-            neg_best.append(tile([P, 2, GROUPS], F32, f"neg_best{h}", "picked0" if h == 1 else None))
+            neg_best.append(tile([P, 2, GROUPS], F32, f"neg_best{h}", "picked0" if h == 0 else None))
             nc.vector.tensor_reduce(
                 neg_best[h][:], a_ps[h][:].rearrange("p r (g j) -> p r g j", j=GROUP), AX.X, ALU.max, negate=True
             )
             a_sb.append(tile([P, 2, Q], F32, f"a_sb{h}"))
             nc.scalar.copy(a_sb[h][:], a_ps[h][:])
         for h in range(2):
-            cut.append(tile([P, 2, GROUPS, GROUP], F32, f"cut{h}"))
+            cut.append(tile([P, 2, GROUPS, GROUP], F32, f"cut{h}", "picked1" if h == 1 else None))
             nc.vector.tensor_tensor(
                 cut[h][:],
                 neg_best[h][:].unsqueeze(3).to_broadcast([P, 2, GROUPS, GROUP]),
@@ -136,15 +131,17 @@ def tile_attend_groupbest_shared_remainder_kernel(tc, query, keys_words, keys_sc
                     stop=(h + r == 2),
                     is_transpose=True,
                 )
-        tgt = tile([P, E], F32, "tgt", "a_sb0")
+
+        tgt = tile([P, E], F32, "tgt", "neg_best1")
         nc.sync.dma_start(tgt[:], target)
+        os_slot = tile([P, PACK], F32, "os_slot", "a_sb0")
+        nc.sync.dma_start(os_slot[:], slot_factor.rearrange("o (p t) -> p (o t)", t=PACK))
 
         v_bf = sb.tile([P, E, PACK], BF16, align_bytes=64)
-        v_codes = sb.tile([P, E], U32, align_bytes=64)
         v_scales = sb.tile([P, E], U8, align_bytes=64)
 
         def gather_values(c):
-            picked = tile([P, I], BF16, f"picked{c}", "pool2" if c == 3 else None)
+            picked = tile([P, I], BF16, f"picked{c}")
             nc.vector.tensor_copy(picked[:], val_pool[c][:].indirect(offsets[:]))
             pairs = picked[:].bitcast(F32)
             turned = ps_v.tile([P, 2, P], F32, name="turned")
@@ -155,34 +152,36 @@ def tile_attend_groupbest_shared_remainder_kernel(tc, query, keys_words, keys_sc
                 turned[:].rearrange("p u e -> p e u"),
             )
 
-        def quantise_values(c):
-            cols = slice(c * P, (c + 1) * P)
+        v_codes = []
+
+        def quantise_values(first_plane, planes, tag):
+            cols = slice(first_plane * P, (first_plane + planes) * P)
+            codes = tile([P, planes * P], U32, f"v_codes{first_plane}", tag)
+            v_codes.append((cols, codes))
             nc.vector.quantize_mx(
-                out=v_codes[:, cols].bitcast(FP8X4),
+                out=codes[:].bitcast(FP8X4),
                 scales=v_scales[:, cols],
                 in_=v_bf[:, cols, :].rearrange("p e t -> p (e t)"),
             )
 
         gather_values(0)
 
-        neg_max = tile([P, 1], F32, "neg_max", "pool0")
-        neg_s = tile([P, I], F32, "neg_s")
-        nc.vector.tensor_scalar(neg_s[:], s_ps[:], minus_one[:], None, ALU.mult, ALU.min, accum_out=neg_max[:])
+        neg_max = tile([P, 1], F32, "neg_max")
+        nc.vector.tensor_reduce(neg_max[:], s_ps[:], AX.X, ALU.max, negate=True)
         prob = sb.tile([P, PACK, P], F32)
-        row_sum = sb.tile([P, 1], F32)
+        row_sum = tile([P, 1], F32, "row_sum", "picked2")
         nc.scalar.activation(
             prob[:], s_ps[:].rearrange("q (s t) -> q t s", t=PACK), ACT.Exp, bias=neg_max[:], accum_out=row_sum[:]
         )
         gather_values(1)
-        row_inv = shared.tile([P, 1], F32, offset=1024, align_bytes=64)
+        row_inv = tile([P, 1], F32, "row_inv")
         nc.vector.reciprocal(row_inv[:], row_sum[:])
-        quantise_values(0)
-        share = sb.tile([P, PACK, P], F32)
-        nc.vector.tensor_scalar(share[:], prob[:], row_inv[:], tiny[:], ALU.mult, ALU.max)
+        share = tile([P, PACK, P], F32, "share", "picked3")
+        nc.vector.tensor_scalar(share[:], prob[:], row_inv[:], TINY, ALU.mult, ALU.max)
         share_sq = sb.tile([P, PACK, P], F32)
         nc.scalar.activation(share_sq[:], prob[:], ACT.Square, scale=row_inv[:])
         warm_root = sb.tile([P, 1], F32)
-        nc.scalar.activation(warm_root[:], row_inv[:], ACT.Abs_reciprocal_sqrt)
+        nc.scalar.activation(warm_root[:], v_bf[:, 2 * P - 1, 0:1], ACT.Abs_reciprocal_sqrt, scale=0.0, bias=half_const[:])
         r_ps = ps.tile([P, PACK, Q], F32)
         for t in range(PACK):
             nc.tensor.transpose(r_ps[:, t, :], share[:, t, :], ident[:])
@@ -191,14 +190,15 @@ def tile_attend_groupbest_shared_remainder_kernel(tc, query, keys_words, keys_sc
             nc.tensor.transpose(sq_ps[:, t, :], share_sq[:, t, :], ident[:])
         gather_values(2)
 
-        group_sum = tile([P, GROUPS, PACK], F32, "group_sum", "pool2")
+        group_sum = tile([P, GROUPS, PACK], F32, "group_sum")
         nc.vector.tensor_reduce(group_sum[:], r_ps[:].rearrange("p t (g j) -> p g t j", j=GROUP), AX.X, ALU.add)
-        group_inv = tile([P, GROUPS, PACK], F32, "group_inv")
-        quantise_values(1)
-        nc.vector.reciprocal(group_inv[:], group_sum[:])
         gather_values(3)
-        factor = tile([P, GROUPS, PACK], F32, "factor", "pool3")
+        group_inv = tile([P, GROUPS, PACK], F32, "group_inv")
+        nc.vector.reciprocal(group_inv[:], group_sum[:])
+        quantise_values(0, 2, "pool3")
+        factor = tile([P, GROUPS, PACK], F32, "factor")
         nc.vector.tensor_tensor(factor[:], group_inv[:], os_slot[:].unsqueeze(1).to_broadcast([P, GROUPS, PACK]), ALU.mult)
+        quantise_values(2, 1, "group_sum")
         w_bf = tile([P, GROUPS, GROUP, PACK], BF16, "w_bf")
         nc.vector.tensor_tensor(
             w_bf[:],
@@ -206,13 +206,12 @@ def tile_attend_groupbest_shared_remainder_kernel(tc, query, keys_words, keys_sc
             factor[:].unsqueeze(2).to_broadcast([P, GROUPS, GROUP, PACK]),
             ALU.mult,
         )
-        quantise_values(2)
+        quantise_values(3, 1, "group_inv")
         w_codes = sb.tile([P, Q], U32, align_bytes=64)
         w_scales = sb.tile([P, Q], U8, align_bytes=64)
         nc.vector.quantize_mx(
             out=w_codes[:].bitcast(FP8X4), scales=w_scales[:], in_=w_bf[:].rearrange("p g j t -> p (g j t)")
         )
-        quantise_values(3)
 
         rest = sb.tile([P, E], F32)
         junk = sb.tile([P, E], F32)
@@ -220,20 +219,21 @@ def tile_attend_groupbest_shared_remainder_kernel(tc, query, keys_words, keys_sc
         for h in range(2):
             cols = slice(h * HALF, (h + 1) * HALF)
             o_ps = ps.tile([P, HALF], F32, name=f"o_ps{h}", tag=f"half{h}")
-            nc.tensor.matmul_mx(
-                out=o_ps[:],
-                lhsT=w_codes[:].bitcast(FP8X4),
-                lhsT_scale=w_scales[:],
-                rhs=v_codes[:, cols].bitcast(FP8X4),
-                rhs_scale=v_scales[:, cols],
-                start=True,
-                stop=True,
-            )
+            for part, codes in v_codes:
+                if part.start // HALF == h:
+                    nc.tensor.matmul_mx(
+                        out=o_ps[:, part.start - h * HALF : part.stop - h * HALF],
+                        lhsT=w_codes[:].bitcast(FP8X4),
+                        lhsT_scale=w_scales[:],
+                        rhs=codes[:].bitcast(FP8X4),
+                        rhs_scale=v_scales[:, part],
+                        start=True,
+                        stop=True,
+                    )
             nc.vector.tensor_tensor(rest[:, cols], tgt[:, cols], o_ps[:], ALU.subtract)
             nc.scalar.activation(junk[:, cols], rest[:, cols], ACT.Square, accum_out=sums[h][:])
-            if h == 0:
-                first = sb.tile([P, 1], F32)
-                nc.scalar.activation(first[:], sums[0][:], ACT.Identity, scale=1.0 / E, bias=half_const[:])
+        first = sb.tile([P, 1], F32)
+        nc.vector.tensor_scalar(first[:], sums[0][:], 1.0 / E, 0.5, ALU.mult, ALU.add)
         inv_root = sb.tile([P, 1], F32)
         nc.scalar.activation(inv_root[:], sums[1][:], ACT.Abs_reciprocal_sqrt, scale=1.0 / E, bias=first[:])
         res = [sb.tile([P, HALF], F32, name=f"res{h}") for h in range(2)]

@@ -33,9 +33,11 @@ def tile_attend_groupbest_shared_remainder_kernel(tc, query, keys_words, keys_sc
         sb = ctx.enter_context(tc.tile_pool(name="sb", bufs=1))
         ps = ctx.enter_context(tc.psum_pool(name="ps", bufs=1))
         ps_v = ctx.enter_context(tc.psum_pool(name="ps_v", bufs=2))
-
+        staged = ctx.enter_context(tc.tile_pool(name="staged", bufs=1))
 
         def tile(shape, dtype, name, tag=None):
+            if isinstance(tag, int):
+                return staged.tile(shape, dtype, name=name, offset=tag, align_bytes=64)
             return sb.tile(shape, dtype, name=name, tag=tag or name, align_bytes=64)
 
         scale_pool = tile([P, T], U8, "scale_pool", "pool2")
@@ -70,7 +72,7 @@ def tile_attend_groupbest_shared_remainder_kernel(tc, query, keys_words, keys_sc
         half_const = tile([P, 1], F32, "half_const")
         nc.vector.memset(half_const[:], 0.5)
 
-        k_words = tile([P, I], U16, "k_words", "pool3")
+        k_words = tile([P, I], U16, "k_words", 2048)
         nc.vector.tensor_copy(k_words[:], word_pool[:].indirect(offsets[:]))
         q_bf = tile([P, Q, PACK], BF16, "q_bf")
         nc.scalar.copy(q_bf[:], q_raw[:].rearrange("p j q -> p q j"))
@@ -99,7 +101,7 @@ def tile_attend_groupbest_shared_remainder_kernel(tc, query, keys_words, keys_sc
                     start=True,
                     stop=True,
                 )
-        val_pool.append(tile([P, T], F32, "val_pool3", "pool3"))
+        val_pool.append(tile([P, T], F32, "val_pool3", 2048))
         nc.sync.dma_start(val_pool[3][:], vals[3 * P : 4 * P, :])
         for h in range(2):
             neg_best.append(tile([P, 2, GROUPS], F32, f"neg_best{h}", "picked0" if h == 0 else None))
@@ -141,10 +143,13 @@ def tile_attend_groupbest_shared_remainder_kernel(tc, query, keys_words, keys_sc
         v_scales = sb.tile([P, E], U8, align_bytes=64)
 
         def gather_values(c):
-            picked = tile([P, I], BF16, f"picked{c}")
+            picked = tile([P, I], BF16, f"picked{c}", 0 if c == 3 else None)
             nc.vector.tensor_copy(picked[:], val_pool[c][:].indirect(offsets[:]))
             pairs = picked[:].bitcast(F32)
-            turned = ps_v.tile([P, 2, P], F32, name="turned")
+            if c == 2:
+                turned = ps.tile([P, 2, P], F32, name="turned2", tag="r_ps")
+            else:
+                turned = ps_v.tile([P, 2, P], F32, name="turned")
             for u in range(2):
                 nc.tensor.transpose(turned[:, u, :], pairs[:, u : I // 2 : 2], ident[:])
             nc.scalar.copy(
@@ -176,9 +181,9 @@ def tile_attend_groupbest_shared_remainder_kernel(tc, query, keys_words, keys_sc
         gather_values(1)
         row_inv = tile([P, 1], F32, "row_inv")
         nc.vector.reciprocal(row_inv[:], row_sum[:])
-        share = tile([P, PACK, P], F32, "share", "picked3")
+        share = tile([P, PACK, P], F32, "share")
         nc.vector.tensor_scalar(share[:], prob[:], row_inv[:], TINY, ALU.mult, ALU.max)
-        share_sq = sb.tile([P, PACK, P], F32)
+        share_sq = tile([P, PACK, P], F32, "share_sq", 0)
         nc.scalar.activation(share_sq[:], prob[:], ACT.Square, scale=row_inv[:])
         warm_root = sb.tile([P, 1], F32)
         nc.scalar.activation(warm_root[:], v_bf[:, 2 * P - 1, 0:1], ACT.Abs_reciprocal_sqrt, scale=0.0, bias=half_const[:])
@@ -193,12 +198,12 @@ def tile_attend_groupbest_shared_remainder_kernel(tc, query, keys_words, keys_sc
         group_sum = tile([P, GROUPS, PACK], F32, "group_sum")
         nc.vector.tensor_reduce(group_sum[:], r_ps[:].rearrange("p t (g j) -> p g t j", j=GROUP), AX.X, ALU.add)
         gather_values(3)
-        group_inv = tile([P, GROUPS, PACK], F32, "group_inv")
+        quantise_values(0, 2, 1024)
+        group_inv = tile([P, GROUPS, PACK], F32, "group_inv", 2048)
         nc.vector.reciprocal(group_inv[:], group_sum[:])
-        quantise_values(0, 2, "pool3")
+        quantise_values(2, 1, 2560)
         factor = tile([P, GROUPS, PACK], F32, "factor")
         nc.vector.tensor_tensor(factor[:], group_inv[:], os_slot[:].unsqueeze(1).to_broadcast([P, GROUPS, PACK]), ALU.mult)
-        quantise_values(2, 1, "group_sum")
         w_bf = tile([P, GROUPS, GROUP, PACK], BF16, "w_bf")
         nc.vector.tensor_tensor(
             w_bf[:],
@@ -206,12 +211,13 @@ def tile_attend_groupbest_shared_remainder_kernel(tc, query, keys_words, keys_sc
             factor[:].unsqueeze(2).to_broadcast([P, GROUPS, GROUP, PACK]),
             ALU.mult,
         )
-        quantise_values(3, 1, "group_inv")
         w_codes = sb.tile([P, Q], U32, align_bytes=64)
         w_scales = sb.tile([P, Q], U8, align_bytes=64)
         nc.vector.quantize_mx(
             out=w_codes[:].bitcast(FP8X4), scales=w_scales[:], in_=w_bf[:].rearrange("p g j t -> p (g j t)")
         )
+
+        quantise_values(3, 1, "factor")
 
         rest = sb.tile([P, E], F32)
         junk = sb.tile([P, E], F32)

@@ -134,7 +134,7 @@ def tile_attend_groupbest_shared_remainder_kernel(tc, query, keys_words, keys_sc
                     is_transpose=True,
                 )
 
-        tgt = tile([P, E], F32, "tgt", "neg_best1")
+        tgt = tile([P, E], F32, "tgt", "a_sb1")
         nc.sync.dma_start(tgt[:], target)
         os_slot = tile([P, PACK], F32, "os_slot", "a_sb0")
         nc.sync.dma_start(os_slot[:], slot_factor.rearrange("o (p t) -> p (o t)", t=PACK))
@@ -179,14 +179,15 @@ def tile_attend_groupbest_shared_remainder_kernel(tc, query, keys_words, keys_sc
             prob[:], s_ps[:].rearrange("q (s t) -> q t s", t=PACK), ACT.Exp, bias=neg_max[:], accum_out=row_sum[:]
         )
         gather_values(1)
-        row_inv = tile([P, 1], F32, "row_inv")
+        row_inv = tile([P, 1], F32, "row_inv", "pool1")
         nc.vector.reciprocal(row_inv[:], row_sum[:])
         share = tile([P, PACK, P], F32, "share")
         nc.vector.tensor_scalar(share[:], prob[:], row_inv[:], TINY, ALU.mult, ALU.max)
         share_sq = tile([P, PACK, P], F32, "share_sq", 0)
-        nc.scalar.activation(share_sq[:], prob[:], ACT.Square, scale=row_inv[:])
+        sq_sum = tile([P, 1], F32, "sq_sum")
+        nc.scalar.activation(share_sq[:], prob[:], ACT.Square, scale=row_inv[:], accum_out=sq_sum[:])
         warm_root = sb.tile([P, 1], F32)
-        nc.scalar.activation(warm_root[:], v_bf[:, 2 * P - 1, 0:1], ACT.Abs_reciprocal_sqrt, scale=0.0, bias=half_const[:])
+        nc.scalar.activation(warm_root[:], sq_sum[:], ACT.Abs_reciprocal_sqrt, bias=half_const[:])
         r_ps = ps.tile([P, PACK, Q], F32)
         for t in range(PACK):
             nc.tensor.transpose(r_ps[:, t, :], share[:, t, :], ident[:])
@@ -195,7 +196,7 @@ def tile_attend_groupbest_shared_remainder_kernel(tc, query, keys_words, keys_sc
             nc.tensor.transpose(sq_ps[:, t, :], share_sq[:, t, :], ident[:])
         gather_values(2)
 
-        group_sum = tile([P, GROUPS, PACK], F32, "group_sum")
+        group_sum = tile([P, GROUPS, PACK], F32, "group_sum", "pool2")
         nc.vector.tensor_reduce(group_sum[:], r_ps[:].rearrange("p t (g j) -> p g t j", j=GROUP), AX.X, ALU.add)
         gather_values(3)
         quantise_values(0, 2, 1024)

@@ -22,25 +22,34 @@ P = 128
 PACK = 4
 GROUP = 8
 GROUPS = Q // GROUP
-PLANES = E // P
-HALF = E // 2
+HALVES = 2
+HALF_TILES = I // P // HALVES
+HALF_COLS = I // 16 // HALVES
+HALF_E = E // HALVES
 TINY = 2.0**-100
 
+STAGED_START = 0
+V_CODES2_AT = 512
+V_CODES0_AT = 1024
 
-def tile_attend_groupbest_shared_remainder_kernel(tc, query, keys_words, keys_scales, lam, slot_factor, vals, target, offs, out):
+
+def tile_attend_groupbest_shared_remainder_kernel(
+    tc, query, keys_words, keys_scales, lam, slot_factor, vals, target, offs, out
+):
     nc = tc.nc
     with ExitStack() as ctx:
         sb = ctx.enter_context(tc.tile_pool(name="sb", bufs=1))
         ps = ctx.enter_context(tc.psum_pool(name="ps", bufs=1))
-        ps_v = ctx.enter_context(tc.psum_pool(name="ps_v", bufs=2))
+        ps_turn = ctx.enter_context(tc.psum_pool(name="ps_turn", bufs=2))
         staged = ctx.enter_context(tc.tile_pool(name="staged", bufs=1))
 
-        def tile(shape, dtype, name, tag=None):
-            if isinstance(tag, int):
-                return staged.tile(shape, dtype, name=name, offset=tag, align_bytes=64)
-            return sb.tile(shape, dtype, name=name, tag=tag or name, align_bytes=64)
+        def tile(shape, dtype, name, buffer=None):
+            return sb.tile(shape, dtype, name=name, tag=buffer or name, align_bytes=64)
 
-        scale_pool = tile([P, T], U8, "scale_pool", "pool2")
+        def tile_at(shape, dtype, name, offset):
+            return staged.tile(shape, dtype, name=name, offset=offset, align_bytes=64)
+
+        scale_pool = tile([P, T], U8, "scale_pool", "plane2")
         nc.gpsimd.memset(scale_pool[:].bitcast(I32), 0)
         offsets = tile([P, I // 16], U16, "offsets")
         nc.sync.dma_start(offsets[:], offs)
@@ -55,82 +64,91 @@ def tile_attend_groupbest_shared_remainder_kernel(tc, query, keys_words, keys_sc
         word_pool = tile([P, T], U16, "word_pool")
         nc.scalar.dma_start(word_pool[:].bitcast(I32), keys_words[0].bitcast(I32))
         q_raw = tile([P, PACK, Q], F32, "q_raw")
-        nc.scalar.dma_start(q_raw[:], query.rearrange("(p j) q -> p j q", j=PACK))
-        seed = tile([P, 1], F32, "seed", "pool0")
-        nc.vector.memset(seed[:], 0.0)
-        seed_bias = tile([P, 1], F32, "seed_bias", "pool1")
-        nc.vector.memset(seed_bias[:], 0.0)
-        warm = tile([P, 1], F32, "warm")
-        nc.scalar.activation(warm[:], seed[:], ACT.Exp, bias=seed_bias[:])
-        val_pool = [tile([P, T], F32, "val_pool0", "pool0")]
-        nc.sync.dma_start(val_pool[0][:], vals[0:P, :])
-        val_pool.append(tile([P, T], F32, "val_pool1", "pool1"))
-        nc.sync.dma_start(val_pool[1][:], vals[P : 2 * P, :])
+        nc.scalar.dma_start(q_raw[:], query.rearrange("(p t) q -> p t q", t=PACK))
+
+        warm_in = tile([P, 1], F32, "warm_in", "plane0")
+        nc.vector.memset(warm_in[:], 0.0)
+        warm_bias = tile([P, 1], F32, "warm_bias", "plane1")
+        nc.vector.memset(warm_bias[:], 0.0)
+        warm_exp = tile([P, 1], F32, "warm_exp")
+        nc.scalar.activation(warm_exp[:], warm_in[:], ACT.Exp, bias=warm_bias[:])
+        val_pool = []
+
+        def load_plane(window):
+            c = len(val_pool)
+            val_pool.append(window)
+            nc.sync.dma_start(window[:], vals[c * P : (c + 1) * P, :])
+
+        load_plane(tile([P, T], F32, "val_pool0", "plane0"))
+        load_plane(tile([P, T], F32, "val_pool1", "plane1"))
 
         ident = tile([P, P], F32, "ident")
         make_identity(nc, ident[:])
-        half_const = tile([P, 1], F32, "half_const")
-        nc.vector.memset(half_const[:], 0.5)
 
-        k_words = tile([P, I], U16, "k_words", 2048)
+        k_words = tile_at([P, I], U16, "k_words", STAGED_START)
         nc.vector.tensor_copy(k_words[:], word_pool[:].indirect(offsets[:]))
         q_bf = tile([P, Q, PACK], BF16, "q_bf")
-        nc.scalar.copy(q_bf[:], q_raw[:].rearrange("p j q -> p q j"))
+        nc.scalar.copy(q_bf[:], q_raw[:].rearrange("p t q -> p q t"))
         q_codes = tile([P, Q], U32, "q_codes")
         q_scales = tile([P, Q], U8, "q_scales")
-        k_scales = [tile([P, I // 2], U8, f"k_scales{h}") for h in range(2)]
-        nc.vector.tensor_copy(k_scales[0][:], scale_pool[:].indirect(offsets[:, 0:16]))
-        nc.vector.quantize_mx(out=q_codes[:].bitcast(FP8X4), scales=q_scales[:], in_=q_bf[:].rearrange("p q j -> p (q j)"))
-        nc.vector.tensor_copy(k_scales[1][:], scale_pool[:].indirect(offsets[:, 16:32]))
-        val_pool.append(tile([P, T], F32, "val_pool2", "pool2"))
-        nc.sync.dma_start(val_pool[2][:], vals[2 * P : 3 * P, :])
+        k_scales = [tile([P, I // HALVES], U8, f"k_scales{h}") for h in range(HALVES)]
+        nc.vector.tensor_copy(k_scales[0][:], scale_pool[:].indirect(offsets[:, :HALF_COLS]))
+        nc.vector.quantize_mx(
+            out=q_codes[:].bitcast(FP8X4), scales=q_scales[:], in_=q_bf[:].rearrange("p q t -> p (q t)")
+        )
+        nc.vector.tensor_copy(k_scales[1][:], scale_pool[:].indirect(offsets[:, HALF_COLS:]))
+        load_plane(tile([P, T], F32, "val_pool2", "plane2"))
 
         lam_row = ps.tile([P, Q], F32)
         nc.tensor.transpose(lam_row[:], lam_col[:].to_broadcast([P, P]), ident[:])
 
         a_ps, a_sb, neg_best, cut = [], [], [], []
-        for h in range(2):
-            a_ps.append(ps.tile([P, 2, Q], F32, name=f"a_ps{h}", tag=f"half{h}"))
-            for r in range(2):
+        for h in range(HALVES):
+            a_ps.append(ps.tile([P, HALF_TILES, Q], F32, name=f"a_ps{h}", tag=f"half{h}"))
+            for r in range(HALF_TILES):
+                first_slot = (HALF_TILES * h + r) * P
                 nc.tensor.matmul_mx(
                     out=a_ps[h][:, r, :],
-                    lhsT=k_words[:, (2 * h + r) * P : (2 * h + r + 1) * P].bitcast(FP4X4),
+                    lhsT=k_words[:, first_slot : first_slot + P].bitcast(FP4X4),
                     lhsT_scale=k_scales[h][:, r * P : (r + 1) * P],
                     rhs=q_codes[:].bitcast(FP8X4),
                     rhs_scale=q_scales[:],
                     start=True,
                     stop=True,
                 )
-        val_pool.append(tile([P, T], F32, "val_pool3", 2048))
-        nc.sync.dma_start(val_pool[3][:], vals[3 * P : 4 * P, :])
-        for h in range(2):
-            neg_best.append(tile([P, 2, GROUPS], F32, f"neg_best{h}", "picked0" if h == 0 else None))
+        load_plane(tile_at([P, T], F32, "val_pool3", STAGED_START))
+
+        grouped = [P, HALF_TILES, GROUPS, GROUP]
+        for h, buffer in enumerate(("picked0", None)):
+            neg_best.append(tile([P, HALF_TILES, GROUPS], F32, f"neg_best{h}", buffer))
             nc.vector.tensor_reduce(
                 neg_best[h][:], a_ps[h][:].rearrange("p r (g j) -> p r g j", j=GROUP), AX.X, ALU.max, negate=True
             )
-            a_sb.append(tile([P, 2, Q], F32, f"a_sb{h}"))
+            a_sb.append(tile([P, HALF_TILES, Q], F32, f"a_sb{h}"))
             nc.scalar.copy(a_sb[h][:], a_ps[h][:])
-        for h in range(2):
-            cut.append(tile([P, 2, GROUPS, GROUP], F32, f"cut{h}", "picked1" if h == 1 else None))
+        for h, buffer in enumerate((None, "picked1")):
+            cut.append(tile(grouped, F32, f"cut{h}", buffer))
             nc.vector.tensor_tensor(
                 cut[h][:],
-                neg_best[h][:].unsqueeze(3).to_broadcast([P, 2, GROUPS, GROUP]),
-                lam_row[:].rearrange("p (g j) -> p g j", j=GROUP).unsqueeze(1).to_broadcast([P, 2, GROUPS, GROUP]),
+                neg_best[h][:].unsqueeze(3).to_broadcast(grouped),
+                lam_row[:].rearrange("p (g j) -> p g j", j=GROUP).unsqueeze(1).to_broadcast(grouped),
                 ALU.mult,
             )
+
         s_ps = ps.tile([P, I], F32)
-        for h in range(2):
-            for r in range(2):
-                cols = slice((2 * h + r) * P, (2 * h + r + 1) * P)
-                nc.tensor.matmul(s_ps[:, cols], a_sb[h][:, r, :], ident[:], start=(h + r == 0), stop=False, is_transpose=True)
-            for r in range(2):
-                cols = slice((2 * h + r) * P, (2 * h + r + 1) * P)
+        for h in range(HALVES):
+            tiles = [(r, slice((HALF_TILES * h + r) * P, (HALF_TILES * h + r + 1) * P)) for r in range(HALF_TILES)]
+            for r, cols in tiles:
+                nc.tensor.matmul(
+                    s_ps[:, cols], a_sb[h][:, r, :], ident[:], start=(cols.start == 0), stop=False, is_transpose=True
+                )
+            for r, cols in tiles:
                 nc.tensor.matmul(
                     s_ps[:, cols],
                     cut[h][:, r, :, :].rearrange("p g j -> p (g j)"),
                     ident[:],
                     start=False,
-                    stop=(h + r == 2),
+                    stop=(cols.stop == I),
                     is_transpose=True,
                 )
 
@@ -139,72 +157,76 @@ def tile_attend_groupbest_shared_remainder_kernel(tc, query, keys_words, keys_sc
         os_slot = tile([P, PACK], F32, "os_slot", "a_sb0")
         nc.sync.dma_start(os_slot[:], slot_factor.rearrange("o (p t) -> p (o t)", t=PACK))
 
-        v_bf = sb.tile([P, E, PACK], BF16, align_bytes=64)
-        v_scales = sb.tile([P, E], U8, align_bytes=64)
-
-        def gather_values(c):
-            picked = tile([P, I], BF16, f"picked{c}", 0 if c == 3 else None)
+        def gather_and_turn(c, picked, turned):
             nc.vector.tensor_copy(picked[:], val_pool[c][:].indirect(offsets[:]))
             pairs = picked[:].bitcast(F32)
-            if c == 2:
-                turned = ps.tile([P, 2, P], F32, name="turned2", tag="r_ps")
-            else:
-                turned = ps_v.tile([P, 2, P], F32, name="turned")
             for u in range(2):
                 nc.tensor.transpose(turned[:, u, :], pairs[:, u : I // 2 : 2], ident[:])
-            nc.scalar.copy(
-                v_bf[:, c * P : (c + 1) * P, :].bitcast(F32),
-                turned[:].rearrange("p u e -> p e u"),
-            )
+            return turned
 
-        v_codes = []
+        def interleave(v_bf, turned):
+            nc.scalar.copy(v_bf.bitcast(F32), turned[:].rearrange("p u e -> p e u"))
 
-        def quantise_values(first_plane, planes, tag):
-            cols = slice(first_plane * P, (first_plane + planes) * P)
-            codes = tile([P, planes * P], U32, f"v_codes{first_plane}", tag)
-            v_codes.append((cols, codes))
+        v_scales = tile([P, E], U8, "v_scales")
+        v_parts = []
+
+        def quantise_values(first_plane, v_bf, codes):
+            cols = slice(first_plane * P, first_plane * P + codes.shape[1])
+            v_parts.append((cols, codes))
             nc.vector.quantize_mx(
-                out=codes[:].bitcast(FP8X4),
-                scales=v_scales[:, cols],
-                in_=v_bf[:, cols, :].rearrange("p e t -> p (e t)"),
+                out=codes[:].bitcast(FP8X4), scales=v_scales[:, cols], in_=v_bf[:].rearrange("p e t -> p (e t)")
             )
 
-        gather_values(0)
+        turned0 = gather_and_turn(0, tile([P, I], BF16, "picked0"), ps_turn.tile([P, 2, P], F32, name="turned"))
 
         neg_max = tile([P, 1], F32, "neg_max")
         nc.vector.tensor_reduce(neg_max[:], s_ps[:], AX.X, ALU.max, negate=True)
-        prob = sb.tile([P, PACK, P], F32)
+        prob = tile([P, PACK, P], F32, "prob")
         row_sum = tile([P, 1], F32, "row_sum", "picked2")
         nc.scalar.activation(
-            prob[:], s_ps[:].rearrange("q (s t) -> q t s", t=PACK), ACT.Exp, bias=neg_max[:], accum_out=row_sum[:]
+            prob[:], s_ps[:].rearrange("q (p t) -> q t p", t=PACK), ACT.Exp, bias=neg_max[:], accum_out=row_sum[:]
         )
-        gather_values(1)
-        row_inv = tile([P, 1], F32, "row_inv", "pool1")
+        turned1 = gather_and_turn(1, tile([P, I], BF16, "picked1"), ps_turn.tile([P, 2, P], F32, name="turned"))
+        row_inv = tile([P, 1], F32, "row_inv", "plane1")
         nc.vector.reciprocal(row_inv[:], row_sum[:])
         share = tile([P, PACK, P], F32, "share")
         nc.vector.tensor_scalar(share[:], prob[:], row_inv[:], TINY, ALU.mult, ALU.max)
-        share_sq = tile([P, PACK, P], F32, "share_sq", 0)
+        share_sq = tile([P, PACK, P], F32, "share_sq")
         sq_sum = tile([P, 1], F32, "sq_sum")
         nc.scalar.activation(share_sq[:], prob[:], ACT.Square, scale=row_inv[:], accum_out=sq_sum[:])
-        warm_root = sb.tile([P, 1], F32)
-        nc.scalar.activation(warm_root[:], sq_sum[:], ACT.Abs_reciprocal_sqrt, bias=half_const[:])
+        v_bf01 = tile([P, 2 * P, PACK], BF16, "v_bf01", "prob")
+        interleave(v_bf01[:, :P, :], turned0)
+        interleave(v_bf01[:, P:, :], turned1)
+        warm_root = tile([P, 1], F32, "warm_root")
+        nc.scalar.activation(warm_root[:], sq_sum[:], ACT.Abs_reciprocal_sqrt)
+
         r_ps = ps.tile([P, PACK, Q], F32)
         for t in range(PACK):
             nc.tensor.transpose(r_ps[:, t, :], share[:, t, :], ident[:])
         sq_ps = ps.tile([P, PACK, Q], F32)
         for t in range(PACK):
             nc.tensor.transpose(sq_ps[:, t, :], share_sq[:, t, :], ident[:])
-        gather_values(2)
+        turned2 = gather_and_turn(
+            2, tile([P, I], BF16, "picked2"), ps.tile([P, 2, P], F32, name="turned2", tag="r_ps")
+        )
+        v_bf2 = tile([P, P, PACK], BF16, "v_bf2")
+        interleave(v_bf2[:], turned2)
 
-        group_sum = tile([P, GROUPS, PACK], F32, "group_sum", "pool2")
+        group_sum = tile([P, GROUPS, PACK], F32, "group_sum", "plane2")
         nc.vector.tensor_reduce(group_sum[:], r_ps[:].rearrange("p t (g j) -> p g t j", j=GROUP), AX.X, ALU.add)
-        gather_values(3)
-        quantise_values(0, 2, 1024)
-        group_inv = tile([P, GROUPS, PACK], F32, "group_inv", 2048)
+        turned3 = gather_and_turn(
+            3, tile([P, I], BF16, "picked3", "share"), ps_turn.tile([P, 2, P], F32, name="turned")
+        )
+        v_bf3 = tile([P, P, PACK], BF16, "v_bf3")
+        interleave(v_bf3[:], turned3)
+        quantise_values(0, v_bf01, tile_at([P, 2 * P], U32, "v_codes0", V_CODES0_AT))
+        group_inv = tile_at([P, GROUPS, PACK], F32, "group_inv", STAGED_START)
         nc.vector.reciprocal(group_inv[:], group_sum[:])
-        quantise_values(2, 1, 2560)
+        quantise_values(2, v_bf2, tile_at([P, P], U32, "v_codes2", V_CODES2_AT))
         factor = tile([P, GROUPS, PACK], F32, "factor")
-        nc.vector.tensor_tensor(factor[:], group_inv[:], os_slot[:].unsqueeze(1).to_broadcast([P, GROUPS, PACK]), ALU.mult)
+        nc.vector.tensor_tensor(
+            factor[:], group_inv[:], os_slot[:].unsqueeze(1).to_broadcast([P, GROUPS, PACK]), ALU.mult
+        )
         w_bf = tile([P, GROUPS, GROUP, PACK], BF16, "w_bf")
         nc.vector.tensor_tensor(
             w_bf[:],
@@ -212,39 +234,40 @@ def tile_attend_groupbest_shared_remainder_kernel(tc, query, keys_words, keys_sc
             factor[:].unsqueeze(2).to_broadcast([P, GROUPS, GROUP, PACK]),
             ALU.mult,
         )
-        w_codes = sb.tile([P, Q], U32, align_bytes=64)
-        w_scales = sb.tile([P, Q], U8, align_bytes=64)
+        w_codes = tile([P, Q], U32, "w_codes")
+        w_scales = tile([P, Q], U8, "w_scales")
         nc.vector.quantize_mx(
             out=w_codes[:].bitcast(FP8X4), scales=w_scales[:], in_=w_bf[:].rearrange("p g j t -> p (g j t)")
         )
+        quantise_values(3, v_bf3, tile([P, P], U32, "v_codes3", "factor"))
 
-        quantise_values(3, 1, "factor")
-
-        rest = sb.tile([P, E], F32)
-        junk = sb.tile([P, E], F32)
-        sums = [sb.tile([P, 1], F32, name=f"sums{h}") for h in range(2)]
-        for h in range(2):
-            cols = slice(h * HALF, (h + 1) * HALF)
-            o_ps = ps.tile([P, HALF], F32, name=f"o_ps{h}", tag=f"half{h}")
-            for part, codes in v_codes:
-                if part.start // HALF == h:
+        rest = tile([P, E], F32, "rest")
+        rest_sq = tile([P, E], F32, "rest_sq")
+        sums = [tile([P, 1], F32, f"sums{h}") for h in range(HALVES)]
+        for h in range(HALVES):
+            half = slice(h * HALF_E, (h + 1) * HALF_E)
+            o_ps = ps.tile([P, HALF_E], F32, name=f"o_ps{h}", tag=f"half{h}")
+            for cols, codes in v_parts:
+                if half.start <= cols.start < half.stop:
                     nc.tensor.matmul_mx(
-                        out=o_ps[:, part.start - h * HALF : part.stop - h * HALF],
+                        out=o_ps[:, cols.start - half.start : cols.stop - half.start],
                         lhsT=w_codes[:].bitcast(FP8X4),
                         lhsT_scale=w_scales[:],
                         rhs=codes[:].bitcast(FP8X4),
-                        rhs_scale=v_scales[:, part],
+                        rhs_scale=v_scales[:, cols],
                         start=True,
                         stop=True,
                     )
-            nc.vector.tensor_tensor(rest[:, cols], tgt[:, cols], o_ps[:], ALU.subtract)
-            nc.scalar.activation(junk[:, cols], rest[:, cols], ACT.Square, accum_out=sums[h][:])
-        first = sb.tile([P, 1], F32)
-        nc.vector.tensor_scalar(first[:], sums[0][:], 1.0 / E, 0.5, ALU.mult, ALU.add)
-        inv_root = sb.tile([P, 1], F32)
-        nc.scalar.activation(inv_root[:], sums[1][:], ACT.Abs_reciprocal_sqrt, scale=1.0 / E, bias=first[:])
-        res = [sb.tile([P, HALF], F32, name=f"res{h}") for h in range(2)]
-        nc.vector.tensor_scalar(res[0][:], rest[:, :HALF], inv_root[:], None, ALU.mult)
-        nc.sync.dma_start(out[:, :HALF], res[0][:])
-        nc.scalar.activation(res[1][:], rest[:, HALF:], ACT.Copy, scale=inv_root[:])
-        nc.scalar.dma_start(out[:, HALF:], res[1][:])
+            nc.vector.tensor_tensor(rest[:, half], tgt[:, half], o_ps[:], ALU.subtract)
+            nc.scalar.activation(rest_sq[:, half], rest[:, half], ACT.Square, accum_out=sums[h][:])
+
+        first_part = tile([P, 1], F32, "first_part")
+        nc.vector.tensor_scalar(first_part[:], sums[0][:], 1.0 / E, 0.5, ALU.mult, ALU.add)
+        inv_root = tile([P, 1], F32, "inv_root")
+        nc.scalar.activation(inv_root[:], sums[1][:], ACT.Abs_reciprocal_sqrt, scale=1.0 / E, bias=first_part[:])
+
+        result = [tile([P, HALF_E], F32, f"result{h}") for h in range(HALVES)]
+        nc.vector.tensor_scalar(result[0][:], rest[:, :HALF_E], inv_root[:], None, ALU.mult)
+        nc.sync.dma_start(out[:, :HALF_E], result[0][:])
+        nc.scalar.activation(result[1][:], rest[:, HALF_E:], ACT.Copy, scale=inv_root[:])
+        nc.scalar.dma_start(out[:, HALF_E:], result[1][:])

from contextlib import ExitStack

import concourse.mybir as mybir
from concourse.masks import make_identity

D, T, I, Q, E = 512, 2048, 512, 128, 512
FLOPS = 2 * D * I * Q + 2 * I * Q * E

F32 = mybir.dt.float32
BF16 = mybir.dt.bfloat16
I32 = mybir.dt.int32
U32 = mybir.dt.uint32
U16 = mybir.dt.uint16
U8 = mybir.dt.uint8
FP8X4 = mybir.dt.float8_e4m3fn_x4
FP4X4 = mybir.dt.float4_e2m1fn_x4
ALU = mybir.AluOpType
ACT = mybir.ActivationFunctionType
AX = mybir.AxisListType

P = 128
PACK = 4
GROUP = 8
GROUPS = Q // GROUP
HALVES = 2
HALF_TILES = I // P // HALVES
HALF_COLS = I // 16 // HALVES
HALF_E = E // HALVES
TINY = 2.0**-100

STAGED_START = 0
V_CODES2_AT = 512
V_CODES0_AT = 1024


def tile_attend_groupbest_shared_remainder_kernel(
    tc, query, keys_words, keys_scales, lam, slot_factor, vals, target, offs, out
):
    nc = tc.nc
    with ExitStack() as ctx:
        sb = ctx.enter_context(tc.tile_pool(name="sb", bufs=1))
        ps = ctx.enter_context(tc.psum_pool(name="ps", bufs=1))
        ps_turn = ctx.enter_context(tc.psum_pool(name="ps_turn", bufs=2))
        staged = ctx.enter_context(tc.tile_pool(name="staged", bufs=1))

        def tile(shape, dtype, name, buffer=None):
            return sb.tile(shape, dtype, name=name, tag=buffer or name, align_bytes=64)

        def tile_at(shape, dtype, name, offset):
            return staged.tile(shape, dtype, name=name, offset=offset, align_bytes=64)

        scale_pool = tile([P, T], U8, "scale_pool", "plane2")
        nc.gpsimd.memset(scale_pool[:].bitcast(I32), 0)
        offsets = tile([P, I // 16], U16, "offsets")
        nc.sync.dma_start(offsets[:], offs)
        lam_col = tile([P, 1], F32, "lam_col")
        with nc.allow_non_contiguous_dma(reason="one factor a partition"):
            nc.scalar.dma_start(lam_col[:], lam.rearrange("o q -> q o"))
        for quad in range(4):
            nc.sync.dma_start(
                scale_pool[32 * quad : 32 * quad + 4, :].bitcast(I32),
                keys_scales[0, 4 * quad : 4 * quad + 4, :].bitcast(I32),
            )
        word_pool = tile([P, T], U16, "word_pool")
        nc.scalar.dma_start(word_pool[:].bitcast(I32), keys_words[0].bitcast(I32))
        q_raw = tile([P, PACK, Q], F32, "q_raw")
        nc.scalar.dma_start(q_raw[:], query.rearrange("(p t) q -> p t q", t=PACK))

        warm_in = tile([P, 1], F32, "warm_in", "plane0")
        nc.vector.memset(warm_in[:], 0.0)
        warm_bias = tile([P, 1], F32, "warm_bias", "plane1")
        nc.vector.memset(warm_bias[:], 0.0)
        warm_exp = tile([P, 1], F32, "warm_exp")
        nc.scalar.activation(warm_exp[:], warm_in[:], ACT.Exp, bias=warm_bias[:])
        val_pool = []

        def load_plane(window):
            c = len(val_pool)
            val_pool.append(window)
            nc.sync.dma_start(window[:], vals[c * P : (c + 1) * P, :])

        load_plane(tile([P, T], F32, "val_pool0", "plane0"))
        load_plane(tile([P, T], F32, "val_pool1", "plane1"))

        ident = tile([P, P], F32, "ident")
        make_identity(nc, ident[:])

        k_words = tile_at([P, I], U16, "k_words", STAGED_START)
        nc.vector.tensor_copy(k_words[:], word_pool[:].indirect(offsets[:]))
        q_bf = tile([P, Q, PACK], BF16, "q_bf")
        nc.scalar.copy(q_bf[:], q_raw[:].rearrange("p t q -> p q t"))
        q_codes = tile([P, Q], U32, "q_codes")
        q_scales = tile([P, Q], U8, "q_scales")
        k_scales = [tile([P, I // HALVES], U8, f"k_scales{h}") for h in range(HALVES)]
        nc.vector.tensor_copy(k_scales[0][:], scale_pool[:].indirect(offsets[:, :HALF_COLS]))
        nc.vector.quantize_mx(
            out=q_codes[:].bitcast(FP8X4), scales=q_scales[:], in_=q_bf[:].rearrange("p q t -> p (q t)")
        )
        nc.vector.tensor_copy(k_scales[1][:], scale_pool[:].indirect(offsets[:, HALF_COLS:]))
        load_plane(tile([P, T], F32, "val_pool2", "plane2"))

        lam_row = ps.tile([P, Q], F32)
        nc.tensor.transpose(lam_row[:], lam_col[:].to_broadcast([P, P]), ident[:])

        a_ps, a_sb, neg_best, cut = [], [], [], []
        for h in range(HALVES):
            a_ps.append(ps.tile([P, HALF_TILES, Q], F32, name=f"a_ps{h}", tag=f"half{h}"))
            for r in range(HALF_TILES):
                first_slot = (HALF_TILES * h + r) * P
                nc.tensor.matmul_mx(
                    out=a_ps[h][:, r, :],
                    lhsT=k_words[:, first_slot : first_slot + P].bitcast(FP4X4),
                    lhsT_scale=k_scales[h][:, r * P : (r + 1) * P],
                    rhs=q_codes[:].bitcast(FP8X4),
                    rhs_scale=q_scales[:],
                    start=True,
                    stop=True,
                )
        load_plane(tile_at([P, T], F32, "val_pool3", STAGED_START))

        grouped = [P, HALF_TILES, GROUPS, GROUP]
        for h, buffer in enumerate(("picked0", None)):
            neg_best.append(tile([P, HALF_TILES, GROUPS], F32, f"neg_best{h}", buffer))
            nc.vector.tensor_reduce(
                neg_best[h][:], a_ps[h][:].rearrange("p r (g j) -> p r g j", j=GROUP), AX.X, ALU.max, negate=True
            )
            a_sb.append(tile([P, HALF_TILES, Q], F32, f"a_sb{h}"))
            nc.scalar.copy(a_sb[h][:], a_ps[h][:])
        for h, buffer in enumerate((None, "picked1")):
            cut.append(tile(grouped, F32, f"cut{h}", buffer))
            nc.vector.tensor_tensor(
                cut[h][:],
                neg_best[h][:].unsqueeze(3).to_broadcast(grouped),
                lam_row[:].rearrange("p (g j) -> p g j", j=GROUP).unsqueeze(1).to_broadcast(grouped),
                ALU.mult,
            )

        s_ps = ps.tile([P, I], F32)
        for h in range(HALVES):
            tiles = [(r, slice((HALF_TILES * h + r) * P, (HALF_TILES * h + r + 1) * P)) for r in range(HALF_TILES)]
            for r, cols in tiles:
                nc.tensor.matmul(
                    s_ps[:, cols], a_sb[h][:, r, :], ident[:], start=(cols.start == 0), stop=False, is_transpose=True
                )
            for r, cols in tiles:
                nc.tensor.matmul(
                    s_ps[:, cols],
                    cut[h][:, r, :, :].rearrange("p g j -> p (g j)"),
                    ident[:],
                    start=False,
                    stop=(cols.stop == I),
                    is_transpose=True,
                )

        tgt = tile([P, E], F32, "tgt", "a_sb1")
        nc.sync.dma_start(tgt[:], target)
        os_slot = tile([P, PACK], F32, "os_slot", "a_sb0")
        nc.sync.dma_start(os_slot[:], slot_factor.rearrange("o (p t) -> p (o t)", t=PACK))

        def gather_and_turn(c, picked, turned):
            nc.vector.tensor_copy(picked[:], val_pool[c][:].indirect(offsets[:]))
            pairs = picked[:].bitcast(F32)
            for u in range(2):
                nc.tensor.transpose(turned[:, u, :], pairs[:, u : I // 2 : 2], ident[:])
            return turned

        def interleave(v_bf, turned):
            nc.scalar.copy(v_bf.bitcast(F32), turned[:].rearrange("p u e -> p e u"))

        v_scales = tile([P, E], U8, "v_scales")
        v_parts = []

        def quantise_values(first_plane, v_bf, codes):
            cols = slice(first_plane * P, first_plane * P + codes.shape[1])
            v_parts.append((cols, codes))
            nc.vector.quantize_mx(
                out=codes[:].bitcast(FP8X4), scales=v_scales[:, cols], in_=v_bf[:].rearrange("p e t -> p (e t)")
            )

        turned0 = gather_and_turn(0, tile([P, I], BF16, "picked0"), ps_turn.tile([P, 2, P], F32, name="turned"))

        neg_max = tile([P, 1], F32, "neg_max")
        nc.vector.tensor_reduce(neg_max[:], s_ps[:], AX.X, ALU.max, negate=True)
        prob = tile([P, PACK, P], F32, "prob")
        row_sum = tile([P, 1], F32, "row_sum", "picked2")
        nc.scalar.activation(
            prob[:], s_ps[:].rearrange("q (p t) -> q t p", t=PACK), ACT.Exp, bias=neg_max[:], accum_out=row_sum[:]
        )
        turned1 = gather_and_turn(1, tile([P, I], BF16, "picked1"), ps_turn.tile([P, 2, P], F32, name="turned"))
        row_inv = tile([P, 1], F32, "row_inv", "plane1")
        nc.vector.reciprocal(row_inv[:], row_sum[:])
        share = tile([P, PACK, P], F32, "share")
        nc.vector.tensor_scalar(share[:], prob[:], row_inv[:], TINY, ALU.mult, ALU.max)
        share_sq = tile([P, PACK, P], F32, "share_sq")
        sq_sum = tile([P, 1], F32, "sq_sum")
        nc.scalar.activation(share_sq[:], prob[:], ACT.Square, scale=row_inv[:], accum_out=sq_sum[:])
        v_bf01 = tile([P, 2 * P, PACK], BF16, "v_bf01", "prob")
        interleave(v_bf01[:, :P, :], turned0)
        interleave(v_bf01[:, P:, :], turned1)
        warm_root = tile([P, 1], F32, "warm_root")
        nc.scalar.activation(warm_root[:], sq_sum[:], ACT.Abs_reciprocal_sqrt)

        r_ps = ps.tile([P, PACK, Q], F32)
        for t in range(PACK):
            nc.tensor.transpose(r_ps[:, t, :], share[:, t, :], ident[:])
        sq_ps = ps.tile([P, PACK, Q], F32)
        for t in range(PACK):
            nc.tensor.transpose(sq_ps[:, t, :], share_sq[:, t, :], ident[:])
        turned2 = gather_and_turn(
            2, tile([P, I], BF16, "picked2"), ps.tile([P, 2, P], F32, name="turned2", tag="r_ps")
        )
        v_bf2 = tile([P, P, PACK], BF16, "v_bf2")
        interleave(v_bf2[:], turned2)

        group_sum = tile([P, GROUPS, PACK], F32, "group_sum", "plane2")
        nc.vector.tensor_reduce(group_sum[:], r_ps[:].rearrange("p t (g j) -> p g t j", j=GROUP), AX.X, ALU.add)
        turned3 = gather_and_turn(
            3, tile([P, I], BF16, "picked3", "share"), ps_turn.tile([P, 2, P], F32, name="turned")
        )
        v_bf3 = tile([P, P, PACK], BF16, "v_bf3")
        interleave(v_bf3[:], turned3)
        quantise_values(0, v_bf01, tile_at([P, 2 * P], U32, "v_codes0", V_CODES0_AT))
        group_inv = tile_at([P, GROUPS, PACK], F32, "group_inv", STAGED_START)
        nc.vector.reciprocal(group_inv[:], group_sum[:])
        quantise_values(2, v_bf2, tile_at([P, P], U32, "v_codes2", V_CODES2_AT))
        factor = tile([P, GROUPS, PACK], F32, "factor")
        nc.vector.tensor_tensor(
            factor[:], group_inv[:], os_slot[:].unsqueeze(1).to_broadcast([P, GROUPS, PACK]), ALU.mult
        )
        w_bf = tile([P, GROUPS, GROUP, PACK], BF16, "w_bf")
        nc.vector.tensor_tensor(
            w_bf[:],
            sq_ps[:].rearrange("p t (g j) -> p g j t", j=GROUP),
            factor[:].unsqueeze(2).to_broadcast([P, GROUPS, GROUP, PACK]),
            ALU.mult,
        )
        w_codes = tile([P, Q], U32, "w_codes")
        w_scales = tile([P, Q], U8, "w_scales")
        nc.vector.quantize_mx(
            out=w_codes[:].bitcast(FP8X4), scales=w_scales[:], in_=w_bf[:].rearrange("p g j t -> p (g j t)")
        )
        quantise_values(3, v_bf3, tile([P, P], U32, "v_codes3", "factor"))

        rest = tile([P, E], F32, "rest")
        rest_sq = tile([P, E], F32, "rest_sq")
        sums = [tile([P, 1], F32, f"sums{h}") for h in range(HALVES)]
        for h in range(HALVES):
            half = slice(h * HALF_E, (h + 1) * HALF_E)
            o_ps = ps.tile([P, HALF_E], F32, name=f"o_ps{h}", tag=f"half{h}")
            for cols, codes in v_parts:
                if half.start <= cols.start < half.stop:
                    nc.tensor.matmul_mx(
                        out=o_ps[:, cols.start - half.start : cols.stop - half.start],
                        lhsT=w_codes[:].bitcast(FP8X4),
                        lhsT_scale=w_scales[:],
                        rhs=codes[:].bitcast(FP8X4),
                        rhs_scale=v_scales[:, cols],
                        start=True,
                        stop=True,
                    )
            nc.vector.tensor_tensor(rest[:, half], tgt[:, half], o_ps[:], ALU.subtract)
            nc.scalar.activation(rest_sq[:, half], rest[:, half], ACT.Square, accum_out=sums[h][:])

        first_part = tile([P, 1], F32, "first_part")
        nc.vector.tensor_scalar(first_part[:], sums[0][:], 1.0 / E, 0.5, ALU.mult, ALU.add)
        inv_root = tile([P, 1], F32, "inv_root")
        nc.scalar.activation(inv_root[:], sums[1][:], ACT.Abs_reciprocal_sqrt, scale=1.0 / E, bias=first_part[:])

        result = [tile([P, HALF_E], F32, f"result{h}") for h in range(HALVES)]
        nc.vector.tensor_scalar(result[0][:], rest[:, :HALF_E], inv_root[:], None, ALU.mult)
        nc.sync.dma_start(out[:, :HALF_E], result[0][:])
        nc.scalar.activation(result[1][:], rest[:, HALF_E:], ACT.Copy, scale=inv_root[:])
        nc.scalar.dma_start(out[:, HALF_E:], result[1][:])
